import numpy as np, ml_dtypes
CORES = [66,74,82,90,194,202,210,218]
N = 8
import mx_ref
BF = ml_dtypes.bfloat16
def tile(rs):
    return np.stack(rs, axis=2).reshape(128, -1).astype(BF)
def pick(q, e):
    c = np.concatenate([q[0].reshape(128, -1, 4), np.zeros((128, 1, 4), np.uint8)], axis=1); s = np.concatenate([q[1], np.ones((16, 1), np.uint8)], axis=1)
    return (np.ascontiguousarray(c[:, e].reshape(128, -1)), np.ascontiguousarray(s[:, e]))
def join(*qs):
    return (np.concatenate([q[0] for q in qs], axis=1), np.concatenate([q[1] for q in qs], axis=1))
def put(q, e, v):
    c, s = q[0].reshape(128, -1, 4).copy(), q[1].copy(); c[:, e] = v[0].reshape(128, -1, 4); s[:, e] = v[1]
    return (c.reshape(128, -1), s)
def pk(c, s):
    return (np.ascontiguousarray(c), mx_ref.live(s))
def emit(q):
    return q[0], q[1]
def packed(v, rng):
    q = [mx_ref.quantize(np.ascontiguousarray(v[r])) for r in range(N)]
    return np.stack([a for a, b in q]), np.stack([mx_ref.plane(b, rng) for a, b in q])
def values_of_codes():
    e, c = np.zeros((128, 128, 4), np.float32), np.zeros((128, 2, 4), np.uint8)
    e[np.arange(128), np.arange(128), 0] = 1
    c[:127, :, 0] = np.arange(256).reshape(2, 128).T[:127]
    return mx_ref.matmul(mx_ref.quantize(e.reshape(128, 512).astype(BF)), (c.reshape(128, 8), np.full((16, 2), 127, np.uint8))).T.reshape(-1).astype(np.float64)
CODE_VALUE, SCALE_VALUE = values_of_codes(), 2.0 ** (np.arange(256) - 127.0)
def decode(q):
    return (CODE_VALUE[q[0]].reshape(16, 8, -1, 4) * SCALE_VALUE[q[1]][:, None, :, None] + 0.0).reshape(128, -1).astype(np.float32)
def f(rng, *shape):
    return mx_ref.flush((rng.standard_normal(shape, dtype=np.float32) * np.exp2(rng.integers(-2, 3, shape[:-1] + (1,)))).astype(BF))
def wide(rng, *shape, cols=0):
    v = rng.standard_normal(shape, dtype=np.float32) * np.exp2(rng.integers(-12, 13, shape)).astype(np.float32)
    if cols: v *= np.repeat(np.exp2(rng.integers(-cols, cols + 1, shape[:-2] + (1, shape[-1] // 4))) * (rng.random(shape[:-2] + (1, shape[-1] // 4)) > 0.0625), 4, axis=-1).astype(np.float32)
    return mx_ref.flush(v.astype(BF))
C, E, K = 288, 4, 72
STEP = [1, 2, 4]
def numbers_of(rng):
    return {"x": np.array(f(rng, N, 128, 4 * C)), "u": np.array(f(rng, N, 128, 512)), "v": np.array(f(rng, N, 128, 512))}
def layers(rng):
    return np.array(f(rng, N, 128, 2048)).reshape(N, 8, 16, 4, 8, 16, 4)
def held(w, parts):
    for i in parts:
        w[:, :, i] = 0
        w[:, :, :, :, :, i] = 0
    for i in parts:
        for g in range(8):
            for b in range(4): w[:, g, i, b, g, i, b] = 64
    return w
def weights(rng, w):
    c, p = packed(np.ascontiguousarray(w).reshape(N, 128, 2048), rng)
    return {"wc": c, "ws": p}
def setup_inputs(rng):
    return {**numbers_of(rng), **weights(rng, layers(rng))}
def setup_inputs_ties(rng):
    d = numbers_of(rng)
    x = d["x"].astype(np.float32).reshape(N, 8, 16, C, 4)
    x[:, :, 0] = 0
    x[:, :, 0, :, 0] = rng.integers(0, 4, (N, 8, C))
    z = (N, 8, 8, C, 4)
    x[:, :, 8:] = (2 * rng.integers(0, 8, z) + 1) * (2.0 * rng.integers(0, 2, z) - 1.0) * np.exp2(-1.0 * rng.integers(12, 19, z))
    x[:, :, 8, :, 0] = 1.96875
    u = d["u"].reshape(N, 128, 128, 4)
    u[:, :, ::16] = 0
    o = rng.permutation(N)
    for r in range(N):
        for h in range(0, 128, 16): u[r, h, h, 0] = 0.0 if r == o[0] else -1.0 if r == o[1] else 1.0
    w = layers(rng)
    w[:, :, 8, :, :, :, 0] = 0
    for r in o[3::2]:
        k = (r + STEP[0]) % N
        w[k, :, :, :, :, 8:] = 0
        for g in range(8):
            x[r, g, 8, :, 0] = 1.125
            x[r, g, 9, :, 0] = (3 + 2 * (g % 2)) * 2.0 ** (-14 - g // 2)
            u[r, 16 * g + 9, 16 * g, 0] = 1.0
            w[k, g, 8, 0, g, 8, 0] = 56
            w[k, g, 9, 0, g, 9, 0] = 32
    return {"x": x.reshape(N, 128, 4 * C).astype(BF), "u": u.reshape(N, 128, 512), "v": d["v"], **weights(rng, held(w, [0]))}
def setup_inputs_near(rng):
    d = numbers_of(rng)
    x = d["x"].astype(np.float32).reshape(N, 8, 16, C, 4)
    x[:, :, 0] = 0
    x[:, :, 8:] = 0
    x[:, :, 0, :, 0] = rng.integers(0, 2, (N, 8, C)) * 2.0 - 1.0
    s = rng.integers(0, 16, (N, 8, C))
    x[:, :, 8] = ((s[:, :, :, None] >> np.arange(4)) & 1) * np.exp2(np.arange(4) - 23.0)
    x[:, :, 11, :, 0] = 2.0 ** -10
    u = d["u"].reshape(N, 128, 128, 4)
    u[:, :, ::16] = 0
    o = rng.permutation(N) % 4
    for r in range(N):
        k = 1.0 if o[r] == 0 else 2.0 ** -30
        if o[r] == 2:
            x[r, :, 0] = 0
            x[r, :, 11] = 0
            for g in rng.permutation(8)[:4]: x[r, g, 0, rng.integers(C), 0] = 2.0 ** 16 * rng.choice([-1.0, 1.0])
        if o[r] == 3:
            x[r, :, 0] = 0
            x[r, :, 8:] = 0
            x[r, :, 10, :, 0] = rng.integers(-4, 5, (8, C)) * 2.0 ** -30
        for h in range(0, 128, 16):
            if o[r] < 2:
                u[r, h, h, 0] = k
                u[r, h + 11, h, 0] = k
            if o[r] == 2: u[r, h, h, 0] = 1.0
            if o[r] < 3: u[r, h + 8, h] = k
            else: u[r, h + 10, h, 0] = k
    w = held(layers(rng), [0, 8, 9, 10, 11, 12, 13, 14, 15])
    return {"x": x.reshape(N, 128, 4 * C).astype(BF), "u": u.reshape(N, 128, 512), "v": d["v"], **weights(rng, w)}
def setup_inputs_huge(rng):
    d = numbers_of(rng)
    o = rng.permutation(N)
    x = (0.8 + 0.2 * rng.random((N, 8, 16, C, 4))) * 1.4 * 2.0 ** 25
    c = rng.integers(0, 2, (N, 1, 1, C, 1)) * 2.0 - 1.0
    c[o < N // 2] = -1.0
    u = d["u"].reshape(N, 128, 128, 4)
    for r in range(N):
        a = 2.0 ** 30 * (1.0 - 0.1 * rng.random((128, 8, 4))) * (rng.permutation(8) % 2 * 2.0 - 1.0)[None, :, None]
        u[r, :, ::16] = a.astype(np.float32).astype(BF)
    w = np.zeros((N, 128, 4, 128, 4), np.float32)
    i = np.arange(128)
    for b in range(4): w[:, i, b, i, b] = 8
    return {"x": (x * c).astype(np.float32).reshape(N, 128, 4 * C).astype(BF), "u": u.reshape(N, 128, 512), "v": d["v"], **weights(rng, w.astype(BF))}
def setup_inputs_ends(rng):
    d = numbers_of(rng)
    e = rng.permutation(N)
    a = np.float32(1.9375 * 2.0 ** 25)
    x = d["x"].astype(np.float32).reshape(N, 8, 16, C, 4)
    u = d["u"].reshape(N, 128, 128, 4)
    u[:, :, ::16] = (2.0 ** 30 * rng.choice([-1.0, 1.0], (N, 1, 8, 1))).astype(np.float32).astype(BF)
    for r in range(N):
        if r == e[0]: x[r] = -a
        elif r == e[1]: x[r] = a * rng.choice([-1.0, 1.0], (1, 1, C, 1))
        elif r == e[2]: x[r] = a * rng.choice([-1.0, 1.0], (8, 16, C, 4))
        elif r == e[3]:
            x[r, :, 8:] = 0
            x[r, :, 8, :, 0] = rng.integers(-1, 2, (8, C)) * 2.0 ** -30
            u[r, :, ::16] = 0
            for h in range(0, 128, 16): u[r, h + 8, h, 0] = 2.0 ** -30
        else: x[r] = -a * rng.choice([0.5, 1.0], (8, 16, C, 4))
    w = layers(rng).astype(np.float32) * np.float32(2.0 ** -10)
    w[:, :, :, :, :, 8:] = 0
    d["v"] = (np.where(d["v"] < 0, -1.0, 1.0) * np.where(rng.permutation(N) % 2, 2.0 ** -30, 2.0 ** 30)[:, None, None]).astype(np.float32).astype(BF)
    return {"x": x.reshape(N, 128, 4 * C).astype(BF), "u": u.reshape(N, 128, 512), "v": d["v"], **weights(rng, mx_ref.flush(w.astype(BF)))}
def setup_inputs_spread(rng):
    d = setup_inputs(rng)
    d["x"] = np.clip(wide(rng, N, 128, 4 * C, cols=3).astype(np.float32), -65536.0, 65536.0).astype(BF)
    return d
def check_inputs(d):
    b = []
    for k in ("x", "u", "v"):
        a = np.abs(d[k].astype(np.float32))
        if not (np.isfinite(a).all() and ((a == 0) | (a >= 2.0 ** -30) & (a <= 2.0 ** 30)).all()): b.append("a value of " + k)
    none, least, most = [emit(mx_ref.quantize(np.full((128, 16), k, np.float32).astype(BF)))[1][0, 0] for k in (0.0, 2.0 ** -30, 2.0 ** 30)]
    top = 0.0
    for r in range(N):
        if ((d["wc"][r] == 0x7F) | (d["wc"][r] == 0xFF)).any(): b.append("wc: a code that is no number")
        s = mx_ref.live(d["ws"][r])
        if ((s != none) & ((s < least) | (s > most))).any(): b.append("ws: a scale out of range")
        w = np.abs(decode(pk(d["wc"][r], d["ws"][r])).astype(np.float64)).reshape(128, 512, 4)
        top = max(top, float(np.max(np.sum(w, axis=(0, 2)))))
    g = min(2.5 + 0.02 * top, 1e60)
    if not g * g * g * float(np.max(np.abs(d["x"].astype(np.float32)))) <= 2.0 ** 30: b.append("x and W: the bound of what they make")
    return b
def reference(x, u, v, wc, ws):
    qu = [mx_ref.quantize(u[r]) for r in range(N)]
    lay = [[pick(pk(wc[r], ws[r]), np.arange(128 * b, 128 * b + 128)) for b in range(4)] for r in range(N)]
    now = [x[r] for r in range(N)]
    for t in range(len(STEP)):
        first = np.arange(t % 2, 8, 2)
        second = (first + 1) % 8
        made = []
        for r in range(N):
            q = mx_ref.quantize(now[r])
            s = mx_ref.matmul(qu[r], q)[::16] + np.float32(0.0)
            o = np.argsort(-s, axis=1, kind="stable")[:, None, :, None]
            a = np.take_along_axis(decode(q).reshape(8, 16, C, 4), o, axis=2).reshape(8, 16, K, E, 4)
            m = np.max(a, axis=3)
            qm = mx_ref.quantize(np.ascontiguousarray(m.reshape(128, 4 * K)).astype(BF))
            back = mx_ref.quantize(tile([mx_ref.matmul(w, qm) * np.float32(0.015625) for w in lay[(r + STEP[t]) % N]]))
            p = decode(back).reshape(8, 16, K, 4)
            c = mx_ref.matmul(qu[r], back)[::16] + np.float32(0.0)
            swap = c[first] < c[second]
            source = np.zeros((8, K), np.int64)
            source[first] = np.where(swap, second[:, None], first[:, None])
            source[second] = np.where(swap, first[:, None], second[:, None])
            away = (a - m[:, :, :, None]).transpose(0, 2, 1, 3, 4)[source, np.arange(K)].transpose(0, 2, 1, 3, 4)
            new = np.zeros((8, 16, C, 4), np.float32)
            np.put_along_axis(new, o, (away + p[:, :, :, None]).reshape(8, 16, C, 4), axis=2)
            made.append(new.reshape(128, 4 * C).astype(BF))
        now = made
    y = np.zeros((N, 128, C), np.float32)
    oc, osc = np.zeros((N, 128, 4 * C), np.uint8), np.zeros((N, 16, C), np.uint8)
    for r in range(N):
        q = mx_ref.quantize(now[r])
        y[r] = mx_ref.matmul(mx_ref.quantize(v[r]), q)
        oc[r], osc[r] = emit(q)
    return {"y": y, "oc": oc, "osc": osc}

from concourse.mybir import dt, AluOpType, AxisListType, ActivationFunctionType

A, F = AluOpType, ActivationFunctionType

C, K, N = 288, 72, 8
STEP = [1, 2, 4]
X4, U8, BF, F32, I32, U16 = "float8_e4m3fn_x4", "uint8", "bfloat16", "float32", "int32", "uint16"
KM = 80
REG = [0, 288, 512, 672, 800, 928]

SCRATCH = {}


def _sb(name, n, d):
    SCRATCH[name] = ("sbuf", [128, n], d)


def _mx(name, n):
    _sb("q" + name, n, X4)
    _sb("s" + name, n, U8)


SCRATCH["ps"] = ("psum", [128, 4096], F32)
for _t in range(3):
    _mx("pk%d" % _t, 2 * C)
    _mx("m%d" % _t, 128)
    _mx("lm%d" % _t, KM + 128)
    _mx("z%d" % _t, 128)
    _mx("lz%d" % _t, 216 if _t == 1 else 128)
for _t in range(4):
    _mx("x%d" % _t, C)
    _mx("e%d" % _t, 320)
for _n, _w in (("uu", 128), ("ur", 320), ("vv", 128), ("ww", 512), ("one", 128), ("ct", REG[5])):
    _mx(_n, _w)
for _n, _w, _d in (
        ("xin", 4 * C, BF), ("uin", 512, BF), ("vin", 512, BF), ("xt", 4 * C, BF), ("zero", 864, BF),
        ("pi", 1, I32), ("p2", 2, F32), ("pint", 5, I32), ("pf", 5, F32), ("col", 8, F32),
        ("uoi", 20, I32), ("uo", 20, U16), ("src", 160, I32),
        ("c32", C, F32), ("gid", 128, F32), ("gt", 256, F32), ("csti", 18, F32), ("cst", 18, F32), ("vali", C, BF), ("val", C, BF),
        ("dofi", 4, F32), ("dof", 4, U16), ("mofi", 72, F32), ("mof", 3 * 72, U16), ("two", 2 * C, F32), ("hc", 18, F32),
        ("mask", C, F32), ("rm", C, BF), ("gb", 4 * 320 + 4, BF), ("ones", 512, BF),
        ("sm", 2 * C + 64, F32), ("st", 2 * C, F32), ("ct", 4 * REG[5], BF), ("sg", 8 * 256, BF), ("junk", 10 * 224, BF),
        ("sc", 2 * C, BF), ("rs", 18, F32), ("pre", 18, F32), ("tc", C, F32), ("t1", 18, F32), ("wf", 18, F32), ("wo", 18, U16),
        ("ws2", 2 * C, BF), ("wt", 2 * C, BF), ("ss", 32, BF), ("s1", 32, BF), ("dd", 64, BF), ("d2", 64, BF), ("off", 36, U16),
        ("h0", C, BF), ("mt", 512, BF), ("mp", 2 * C, BF), ("mx", 8 * C, BF),
        ("aw", 8 * C, F32), ("zt", 512, BF), ("gg", C, F32), ("g2", C, F32), ("ki", 18, I32), ("kq", 18, U16),
        ("bi", 18, I32), ("kb", 18, U16), ("vf", 144, F32), ("swp", 144, F32), ("ix", C, F32), ("it", C, F32),
        ("idx", 18, U16), ("pp", 4 * KM, BF), ("px", 4 * C, BF), ("yo", C, F32)):
    _sb(_n, _w, _d)

SEMAPHORES = ["cv", "cs", "cp", "cg", "lx", "lu", "lw", "lv", "sent", "o1", "o2", "dm"] + \
             ["%s%d" % (_n, _t) for _n in ("sm", "am", "az") for _t in range(3)]


def rank_program(g, core, T, topo):
    rank = T.rank_of(core)
    if rank is None:
        return
    eng = {"v": g.vector, "s": g.scalar, "p": g.tensor, "g": g, "y": g.sync}
    csem = {"v": "cv", "s": "cs", "p": "cp", "g": "cg"}
    count = {}
    known = {e: {} for e in eng}
    wrote, read = {}, {}

    def wait(e, tok):
        sem, val, clock = tok[1], tok[2], tok[3]
        if known[e].get(sem, 0) < val:
            eng[e].wait_ge(T.sem[sem], val)
            known[e][sem] = val
        for k2, v2 in clock.items():
            if known[e].get(k2, 0) < v2:
                known[e][k2] = v2

    def op(e, call, r=(), w=(), sem=None, inc=1, acc=False):
        need = []
        for k in r:
            if k in wrote:
                need.append(wrote[k])
            if k.startswith("pb"):
                need += [t for t in read.get(k, []) if t[0] != e]
        for k in w:
            if k in wrote and not acc:
                need.append(wrote[k])
            need += read.get(k, [])
        need.sort(key=lambda t: -t[2])
        for t in need:
            wait(e, t)
        sem = sem or csem[e]
        call().then_inc(T.sem[sem], inc)
        count[sem] = count.get(sem, 0) + inc
        tok = (e, sem, count[sem], dict(known[e]))
        for k in r:
            read.setdefault(k, []).append(tok)
        for k in w:
            wrote[k] = tok
            read[k] = []
        return tok

    V, S, P = g.vector, g.scalar, g.tensor

    def pb(bank, a, b, step=1):
        return T.ps[:, 512 * bank + a:512 * bank + b:step]

    def quant(name, a, b, src, r, w=None):
        op("v", lambda: V.quantize_mx(T["q" + name][:, a:b], T["s" + name][:, a:b], src), r, w or ["q" + name])

    def mm(bank, n, lh, la, rh, ra, start, stop, r):
        op("p", lambda: P.matmul_mx(pb(bank, 0, n), T["q" + lh][:, la:la + 128], T["s" + lh][:, la:la + 128],
                                    T["q" + rh][:, ra:ra + n], T["s" + rh][:, ra:ra + n], start, stop),
           r, ["pb%d" % bank], acc=not start)

    def iota(name, pattern, base, cm, small=True):
        if small:
            op("g", lambda: g.iota(T[name][:], pattern, base, cm, allow_small_or_imprecise_dtypes=True), [], [name])
        else:
            op("g", lambda: g.iota(T[name][:], pattern, base, cm), [], [name])

    def ts(out, in0, s1, s2, o0, o1, r, w):
        if o1 is None:
            op("v", lambda: V.tensor_scalar(out, in0, s1, None, o0), r, w)
        else:
            op("v", lambda: V.tensor_scalar(out, in0, s1, s2, o0, o1), r, w)

    def tt(out, a, b, o, r, w):
        op("v", lambda: V.tensor_tensor(out, a, b, o), r, w)

    def cp(out, a, r, w):
        op("v", lambda: V.tensor_copy(out, a), r, w)

    def tr(out, a, r, w):
        op("v", lambda: V.transpose(out, a), r, w)

    def act(out, a, f, r, w, **kw):
        op("s", lambda: S.activation(out, a, f, **kw), r, w)

    def fill(ap, n, w):
        op("g", lambda: g.iota(ap, [[0, n]], 0, 0, allow_small_or_imprecise_dtypes=True), [], w)

    def send(name, land, a, n, dst, sem, left):
        rid, pid = topo.addr(dst, core)
        m = topo.mask(core, dst)
        wait("g", wrote["q" + name])
        g.remote_dma(T["q" + land][:, a:a + n].bitcast(dt.uint8), T["q" + name][:, 0:n].bitcast(dt.uint8),
                     T.sem[sem], T.sem[left], pid, rid, m)
        g.remote_dma(T["s" + land][:, a:a + n], T["s" + name][:, 0:n], T.sem[sem], T.sem[left], pid, rid, m)
        count[left] = count.get(left, 0) + 2 * len(topo.engines(core, dst))

    def arrived(key, sem, src):
        wrote[key] = ("r", sem, 2 * len(topo.engines(src, core)), {})
        read[key] = []

    op("s", lambda: S.dma_start(T.uin[:], T.u[:]), [], ["uin"], sem="lu", inc=16)
    op("y", lambda: g.sync.dma_start(T.xin[:], T.x[:]), [], ["xin"], sem="lx", inc=16)
    op("y", lambda: g.sync.dma_start(T.qww[:].bitcast(dt.uint8), T.wc[:]), ["xin"], ["qww0"], sem="lw", inc=16)
    op("y", lambda: g.sync.dma_start(T.sww[:], T.ws[:]), [], ["qww"], sem="lw", inc=16)
    op("y", lambda: g.sync.dma_start(T.vin[:], T.v[:]), [], ["vin"], sem="lv", inc=16)

    iota("pi", [[0, 1]], 0, 1, False)
    iota("src", [[1, 160]], 112, 0, False)
    iota("p2", [[1024, 2]], 0, 1)
    iota("uoi", [[112, 2], [32, 5], [0, 2]], 0, 0, False)
    iota("c32", [[0, 9], [2, 32]], 1, 0)
    iota("gid", [[1, 8], [0, 16]], 0, 0)
    for a in (256, 480, 640, 736, 800):
        fill(T.ct[:, 4 * a + 1:4 * a + 128:2], 64, ["ctz%d" % a])
    fill(T.ct[:, 4 * 768:4 * 800], 128, ["ctz768"])
    fill(T.rs[:, 0:2], 2, ["rs0", "rs1"])
    fill(T.zero[:, 0:512], 512, ["zero"])
    iota("csti", [[32, 9], [C, 2]], 0, 0)
    iota("vali", [[32, 9], [0, 2], [1, 16]], -144, 0)
    fill(T.ws2[:], 2 * C, ["ws2"])
    fill(T.ss[:], 32, ["ss"])
    iota("dofi", [[16, 2], [0, 2]], 0, 0)
    iota("two", [[0, 2], [2, C]], 0, 0)
    iota("hc", [[0, 9], [-C, 2]], 0, 0)
    fill(T.mt[:, C:512], 512 - C, ["mtz"])
    iota("mofi", [[1, 4], [16, 18]], 0, 0)
    fill(T.zt[:, C:512], 512 - C, ["ztz"])
    fill(T.zero[:, 512:864], 352, ["zero2"])
    op("v", lambda: V.memset(T.gb[:], 0.0), [], ["gb"])
    for i, bits in enumerate((31, 16, 15, 12, 96)):
        ts(T.pint[:, i:i + 1], T.pi[:], bits, None, A.bitwise_and, None, ["pi"], ["pint%d" % i])
    ts(T.src[:], T.src[:], 127, None, A.bitwise_and, None, ["src"], ["src"])
    cp(T.pf[:], T.pint[:], ["pint%d" % i for i in range(5)], ["pf"])
    ts(T.uoi[:], T.uoi[:], 127, None, A.bitwise_and, None, ["uoi"], ["uoi"])
    act(T.col[:, 0:1], T.pf[:, 1:2], F.Identity, ["pf", "p2"], ["col0"], bias=T.p2[:, 0:1], scale=64.0)
    act(T.col[:, 1:2], T.pf[:, 1:2], F.Identity, ["pf", "p2"], ["col1"], bias=T.p2[:, 1:2], scale=-64.0)
    act(T.col[:, 2:3], T.pf[:, 0:1], F.Identity, ["pf"], ["col2"], scale=-2e27)
    act(T.col[:, 3:4], T.pf[:, 4:5], F.Identity, ["pf"], ["col3"], scale=-0.0625)
    act(T.col[:, 4:5], T.pf[:, 4:5], F.Identity, ["pf"], ["col4"], bias=-1.0, scale=-0.0625)
    act(T.col[:, 5:6], T.pf[:, 1:2], F.Identity, ["pf"], ["col5"], scale=C / 16.0)
    act(T.col[:, 6:7], T.pf[:, 1:2], F.Identity, ["pf"], ["col6"], bias=float(C), scale=-C / 16.0)
    act(T.mask[:], T.c32[:], F.Identity, ["c32", "col2"], ["mask"], bias=T.col[:, 2:3], scale=1e27)
    cp(T.uo[:], T.uoi[:], ["uoi"], ["uo"])
    ts(T.gb[:, 3:640:4], T.src[:], T.col[:, 0:1], None, A.is_equal, None, ["src", "col0", "gb"], ["gb0"])
    ts(T.gb[:, 643:1280:4], T.src[:], T.col[:, 1:2], None, A.is_equal, None, ["src", "col1", "gb"], ["gb1"])

    def ident(b):
        quant("e%d" % b, 0, 320, T.gb[:, 3 - b:3 - b + 1280], ["gb0", "gb1"])
    ident(0)
    quant("uu", 0, 128, T.uin[:], ["uin"])
    act(T.sur[:], T.suu[:].indirect(T.uo[:]), F.Copy, ["quu", "uo"], ["sur"])
    op("v", lambda: V.tensor_copy(T.qur[:].bitcast(dt.uint32), T.quu[:].bitcast(dt.uint32).indirect(T.uo[:])), ["quu", "uo"], ["qur"])
    quant("x0", 0, C, T.xin[:], ["xin"])
    act(T.rm[:], T.c32[:], F.Sign, ["c32"], ["rm"], bias=-1.0)
    for i in range(2):
        act(T.gt[:, 128 * i:128 * i + 128], T.gid[:], F.Abs, ["gid", "col%d" % (3 + i)], ["gt%d" % i], bias=T.col[:, 3 + i:4 + i])
    for t in range(4):
        act(T.ones[:, t:512:4], T.gt[:, 128 * (t // 2):128 * (t // 2) + 128], F.Relu, ["gt%d" % (t // 2)], ["ones%d" % t], bias=1.0, scale=-1.0)
    UR = ["qur", "sur"]
    ZK = ["ctz256", "ctz480", "ctz640", "ctz736", "ctz768", "ctz800"]

    def slot(beta, h):
        reg, t = (9 - beta) // 2, 2 * h + (9 - beta) % 2
        n = C if beta == 9 else 32 * beta
        return T.ct[:, 4 * REG[reg] + t:4 * (REG[reg] + n):4], "ct%d_%d" % (beta, h)

    def spread(src, n, keys, sel, tile):
        for b in range(4):
            o = (4 * sel + b) * C
            act(T.mx[:, o:o + C], src[:, 0:n].indirect(T.mof[:, 72 * tile + 18 * b:72 * tile + 18 * b + 18]), F.Copy,
                keys + ["mof%d" % tile], ["mx%d_%d" % (sel, b)])

    def away(sel):
        for b in range(4):
            o = (4 * sel + b) * C
            tt(T.aw[:, 2 * C * b + sel:2 * C * (b + 1):2], pb(b, 0, C), T.mx[:, o:o + C], A.subtract,
               ["pb%d" % b, "mx%d_%d" % (sel, b)], ["aw%d_%d" % (sel, b)])

    for t in range(3):
        x, pk, m, lm, z, lz = ["%s%d" % (s, t) for s in ("x", "pk", "m", "lm", "z", "lz")]
        helper, client = T.cores[(rank + STEP[t]) % N], T.cores[(rank - STEP[t]) % N]
        for bank, ua in ((0, 0), (2, 0), (1, 192), (3, 192)):
            mm(bank, C, "ur", ua, x, 0, True, True, UR + ["q" + x])
        if t == 0:
            ident(1)
            ident(2)
        srows = [(8, 0), (7, 0), (6, 0), (8, 1), (7, 1), (5, 0), (4, 0)]
        vrows = [(6, 1), (5, 1), (4, 1), (3, 0), (3, 1), (2, 0), (2, 1), (1, 0), (1, 1)]
        tr(T.sm[:, 2 * C:2 * C + 64], pb(0, 224, C), ["pb0"], ["su"])
        for h in range(2):
            tt(T.sm[:, C * h:C * h + C], pb(h, 0, C), T.mask[:], A.min, ["pb%d" % h, "mask"], ["sm%d" % h])
            tr(T.st[:, C * h:C * h + C], T.sm[:, C * h:C * h + C], ["sm%d" % h], ["st%d" % h])

        def sign(i):
            be, h = srows[i]
            a = 2 * C + 32 * be - 224
            col, key = (T.sm[:, a:a + 1], "su") if i < 2 else (T.st[:, C * h + 32 * be:C * h + 32 * be + 1], "st%d" % h)
            act(T.sg[:, 256 * i:256 * i + 32 * be], pb(2 + h, 0, 32 * be), F.Sign, ["pb%d" % (2 + h), key], ["sg%d" % i],
                bias=col, scale=-1.0)

        def relu(i):
            be, h = srows[i]
            view, key = slot(be, h)
            act(view, T.sg[:, 256 * i:256 * i + 32 * be], F.Relu, ["sg%d" % i], [key, "rs%d" % (2 * be + h)],
                accum_out=T.rs[:, 2 * be + h:2 * be + h + 1])
        sign(0)
        for i in range(len(srows)):
            if i + 1 < len(srows):
                sign(i + 1)
            relu(i)
        for h in range(2):
            view, key = slot(9, h)
            tt(view, pb(h, 0, C), T.st[:, C * h:C * h + C], A.is_lt, ["pb%d" % h, "st%d" % h], [key])
        for i, (be, h) in enumerate(vrows):
            view, key = slot(be, h)
            ts(view, pb(h, 0, 32 * be), T.st[:, C * h + 32 * be:C * h + 32 * be + 1], None, A.is_lt, None,
               ["pb%d" % h, "st%d" % h], [key])
            if be > 1:
                act(T.junk[:, 224 * i:224 * i + 32 * be], view, F.Identity, [key], ["junk%d" % i, "rs%d" % (2 * be + h)],
                    accum_out=T.rs[:, 2 * be + h:2 * be + h + 1])
        if t == 0:
            quant("one", 0, 128, T.ones[:], ["ones%d" % i for i in range(4)])
            quant("ct", 800, 928, T.zero[:, 0:512], ["zero"], ["qct1"])
            act(T.cst[:], T.csti[:], F.Identity, ["csti", "pf"], ["cst"], bias=T.pf[:, 0:1])
            act(T.val[:], T.vali[:], F.Identity, ["vali", "pf"], ["val"], bias=T.pf[:, 1:2])
        quant("ct", 0, 512, T.ct[:, 0:2048], ["ct%d_%d" % (be, h) for be in (9, 8, 7, 6) for h in range(2)] + ZK, ["qct0"])
        quant("ct", 512, 832, T.ct[:, 2048:3328], ["ct%d_%d" % (be, h) for be in (5, 4, 3, 2, 1) for h in range(2)] + ZK, ["qct1"])
        for i in range(5):
            mm(4, REG[i + 1] - REG[i], "one", 0, "ct", REG[i], i == 0, i == 4, ["qone", "qct%d" % (i // 2 > 0)])
        for h in range(2):
            view, key = slot(9, h)
            op("v", lambda: V.tensor_tensor_scan(T.sc[:, C * h:C * h + C], T.rm[:], view, 0.0, A.mult, A.add), [key, "rm"], ["sc%d" % h])
        for h in range(2):
            view, key = slot(1, h)
            op("v", lambda: V.tensor_reduce(T.rs[:, 2 + h:3 + h], view, AxisListType.X, A.add), [key], ["rs%d" % (2 + h)])
        for h in range(2):
            tt(T.pre[:, h:18:2], T.cst[:, h:18:2], T.sc[:, C * h + 31:C * h + C:32], A.subtract, ["cst", "sc%d" % h], ["pre%d" % h])
        tr(T.tc[:], pb(4, 0, C), ["pb4"], ["tc"])
        tt(T.t1[:], T.pre[:], T.rs[:], A.subtract, ["pre0", "pre1"] + ["rs%d" % i for i in range(18)], ["t1"])
        tt(T.wf[:], T.tc[:, 0:C:16], T.t1[:], A.add, ["tc", "t1"], ["wf"])
        cp(T.wo[:], T.wf[:], ["wf"], ["wo"])
        cp(T.ws2[:].indirect(T.wo[:]), T.val[:], ["wo", "val"], ["ws2"])
        if t == 0:
            ident(3)
            ts(T.dof[:], T.dofi[:], T.pf[:, 2:3], None, A.add, None, ["dofi", "pf"], ["dof"])
        tr(T.wt[:], T.ws2[:], ["ws2"], ["wt"])
        tt(T.ss[:, 0:18], T.wt[:, 0:2 * C:32], T.wt[:, 16:2 * C:32], A.add, ["wt"], ["ss"])
        tr(T.s1[:], T.ss[:], ["ss"], ["s1"])
        cp(T.dd[:], T.s1[:].indirect(T.dof[:]), ["s1", "dof"], ["dd"])
        tr(T.d2[:], T.dd[:], ["dd"], ["d2"])
        for i in range(2):
            ts(T.off[:, i:36:2], T.d2[:, 32 * i:32 * i + 18], 144.0, None, A.add, None, ["d2"], ["off%d" % i])
        for i in range(2):
            o = T.off[:, 18 * i:18 * i + 18]
            act(T["s" + pk][:, C * i:C * i + C], T["s" + x][:].indirect(o), F.Copy, ["q" + x, "off0", "off1"], ["s%s_%d" % (pk, i)])
            op("v", lambda: V.tensor_copy(T["q" + pk][:, C * i:C * i + C].bitcast(dt.uint32), T["q" + x][:].bitcast(dt.uint32).indirect(o)),
               ["q" + x, "off0", "off1"], ["q%s_%d" % (pk, i)])
        mt = ["mt%d" % i for i in range(4)]

        def unpack(b, i, shift):
            mm(b, C, "e%d" % b, 160 * i + shift, pk, C * i, i == 0, i == 1, ["qe%d" % b, "q%s_%d" % (pk, i), "s%s_%d" % (pk, i)])
        for b, i in ((0, 0), (1, 0), (0, 1), (1, 1), (2, 0), (2, 1), (3, 0), (3, 1)):
            unpack(b, i, 16)
        cp(T.gg[:], T.two[:].indirect(T.wo[:]), ["two", "wo"], ["gg"])
        for b in range(4):
            act(T.h0[:, K * b:K * b + K], pb(b, 0, C, 4), F.Copy, ["pb%d" % b], ["h%d" % b])
        if t == 0:
            quant(lz, 0, 128, T.zero[:, 0:512], ["zero"])
        for b, e in ((0, 1), (1, 1), (0, 2), (1, 2), (0, 3), (2, 1), (1, 3), (2, 2), (3, 1), (2, 3), (3, 2), (3, 3)):
            run = T.h0[:, K * b:K * b + K]
            tt(run if e < 3 else T.mt[:, b:C:4], pb(b, e, C, 4), run, A.max, ["pb%d" % b, "h%d" % b], ["h%d" % b if e < 3 else mt[b]])
        quant(m, 0, 128, T.mt[:], mt + ["mtz", "q" + lz])
        send(m, lm, 0, KM, helper, "am%d" % t, "sm%d" % t)
        wait("y", ("r", "sm%d" % t, count["sm%d" % t], {}))
        for i, (o, a, c, n) in enumerate(((0, 16, 0, 112), (16, 0, C, 112), (112, 0, 0, 16), (0, 112, C, 16))):
            op("y", lambda: g.sync.dma_start(T.mp[o:o + n, c:c + C], T.mt[a:a + n, 0:C]), mt, ["mp%d" % i], sem="dm", inc=16)
        for i in range(3):
            wrote["mp%d" % i] = wrote["mp3"]
        for k in mt:
            read[k] = [tok for tok in read[k] if tok[1] != "dm"] + [wrote["mp3"]]
        if t < 2:
            fill(T.ws2[:], 2 * C, ["ws2"])
        if t == 0:
            ts(T.mof[:, 0:72], T.mofi[:], T.pf[:, 3:4], None, A.add, None, ["mofi", "pf"], ["mof0"])
            quant(lm, KM, KM + 128, T.zero[:, 0:512], ["zero"], ["pad" + lm])
        spread(T.mt, C, mt, 0, 0)
        if t == 1:
            cp(T.ki[:], T.wf[:], ["wf"], ["ki"])
        else:
            tt(T.ki[:], T.wf[:], T.hc[:], A.add, ["wf", "hc"], ["ki"])
        tr(T.g2[:], T.gg[:], ["gg"], ["g2"])
        away(0)
        arrived("q" + lm, "am%d" % t, client)
        for b in range(4):
            mm(4 + b, 128, "ww", 128 * b, lm, 0, True, True, ["qww", "q" + lm, "pad" + lm])
        up = 32 * (t % 2)
        for b in range(4):
            unpack(b, 0, up)
            unpack(b, 1, 32 - up)
        for b in range(2):
            act(T.zt[:, 2 * b + 1:C:4], pb(2 * b + 5, 0, K), F.Copy, ["pb%d" % (2 * b + 5)], ["zt%d" % (2 * b + 1)], scale=0.015625)
            ts(T.zt[:, 2 * b:C:4], pb(2 * b + 4, 0, K), 0.015625, None, A.mult, None, ["pb%d" % (2 * b + 4)], ["zt%d" % (2 * b)])
        quant(z, 0, 128, T.zt[:], ["zt%d" % i for i in range(4)] + ["ztz"])
        za = K if t == 1 else 0
        send(z, lz, za, K, client, "az%d" % t, "sent")
        if t < 2:
            ts(T.mof[:, 72 + 72 * t:144 + 72 * t], T.mofi[:], T.pf[:, 3:4], T.col[:, 5 + t:6 + t], A.add, A.add,
               ["mofi", "pf", "col%d" % (5 + t)], ["mof%d" % (1 + t)])
        spread(T.mp, 2 * C, ["mp%d" % i for i in range(4)], 1, 1 + t % 2)
        ts(T.ki[:], T.ki[:], 2, None, A.arith_shift_right, None, ["ki"], ["ki"])
        cp(T.bi[:], T.g2[:, 0:C:16], ["g2"], ["bi"])
        cp(T.kq[:], T.ki[:], ["ki"], ["kq"])
        ts(T.bi[:], T.bi[:], 3, None, A.arith_shift_right, None, ["bi"], ["bi"])
        if t == 2:
            quant("vv", 0, 128, T.vin[:], ["vin"])
        cp(T.kb[:], T.bi[:], ["bi"], ["kb"])
        if t < 2:
            nz = 216 if t == 0 else 128
            quant("lz%d" % (t + 1), 0, nz, T.zero[:, 0:4 * nz], ["zero", "zero2"])
            quant("lm%d" % (t + 1), KM, KM + 128, T.zero[:, 0:512], ["zero"], ["padlm%d" % (t + 1)])
        away(1)
        arrived("q" + lz, "az%d" % t, helper)
        if t == 1:
            nv = 2 * K
            for bank, ua in ((4, 160), (5, 0)):
                mm(bank, nv, "ur", ua + 32, lz, 0, True, False, UR + ["q" + lz])
                mm(bank, nv, "ur", ua, lz, K, False, True, UR + ["q" + lz])
        else:
            nv = K
            mm(4, 128, "ur", 0, lz, 0, True, True, UR + ["q" + lz])
            mm(5, 128, "ur", 192, lz, 0, True, True, UR + ["q" + lz])
        pbank = (6, 7, 0, 1)
        for b in range(4):
            for i in range(2):
                mm(pbank[b], 128, "e%d" % b, 160 * i + 16, lz, za, i == 0, i == 1, ["qe%d" % b, "q" + lz])
        cp(T.vf[:, 0:nv], pb(4, 0, nv), ["pb4"], ["vf"])
        tt(T.swp[:, 0:nv], pb(5, 0, nv), T.vf[:, 0:nv], A.is_gt, ["pb5", "vf"], ["swp"])
        tt(T.ix[:], T.swp[:, 0:nv].indirect(T.kq[:]), T.gg[:], A.add, ["swp", "kq", "gg"], ["ix"])
        tr(T.it[:], T.ix[:], ["ix"], ["it"])
        cp(T.idx[:], T.it[:, 0:C:16], ["it"], ["idx"])
        for b in range(4):
            for a in ((0, 1), (2,), (3,), ())[b]:
                act(T.pp[:, KM * a:KM * a + K], pb(pbank[a], 0, K), F.Copy, ["pb%d" % pbank[a]], ["pp%d" % a])
            act(T.px[:, C * b:C * b + C], T.pp[:, KM * b:KM * b + K].indirect(T.kb[:]), F.Copy, ["pp%d" % b, "kb"], ["px%d" % b])
            tt(T.xt[:, b:4 * C:4], T.aw[:, 2 * C * b:2 * C * (b + 1)].indirect(T.idx[:]), T.px[:, C * b:C * b + C], A.add,
               ["aw0_%d" % b, "aw1_%d" % b, "idx", "px%d" % b], ["xt%d" % b])
        quant("x%d" % (t + 1), 0, C, T.xt[:], ["xt%d" % i for i in range(4)])

    mm(6, C, "vv", 0, "x3", 0, True, True, ["qvv", "qx3"])
    op("y", lambda: g.sync.dma_start(T.oc[:], T.qx3[:].bitcast(dt.uint8)), ["qx3"], [], sem="o1", inc=16)
    for k in range(4):
        e = "y" if k < 2 else "s"
        op(e, lambda: eng[e].dma_start(T.osc[4 * k:4 * k + 4, :], T.sx3[32 * k:32 * k + 4, :]), ["qx3"], [],
           sem="o1" if k < 2 else "o2", inc=16)
    cp(T.yo[:], pb(6, 0, C), ["pb6"], ["yo"])
    op("s", lambda: S.dma_start(T.y[:], T.yo[:]), ["yo"], [], sem="o2", inc=16)
    for sem in ("cv", "cs", "cp", "cg", "lx", "lu", "lw", "lv", "sent", "o1", "o2", "dm", "sm0", "sm1", "sm2"):
        g.wait_ge(T.sem[sem], count[sem])
